import numpy as np
import ml_dtypes


def mxq(x, axis, fmt="e4m3"):
    dtype, down = {"e4m3": (ml_dtypes.float8_e4m3fn, 7), "e5m2": (ml_dtypes.float8_e5m2, 14)}[fmt]
    v = np.moveaxis(np.asarray(x, np.float32).astype(ml_dtypes.bfloat16).astype(np.float64), axis, -1)
    blocks = v.reshape(v.shape[:-1] + (-1, 32))
    amax = np.abs(blocks).max(-1, keepdims=True)
    byte = np.maximum(np.where(amax > 0, np.frexp(amax)[1] - 1 + 127, 0) - down, 1)
    scale = np.exp2(byte - 127.0)
    codes = (blocks / scale).astype(np.float32).astype(dtype).astype(np.float64)
    return np.moveaxis((codes * scale).reshape(v.shape), -1, axis)


WIDE = False


def mx_kscale(k):
    if not WIDE:
        return np.ones(k)
    levels = np.array([10, -10, 5, -5, 0])
    if k % 512:
        return np.exp2(np.random.permutation(np.resize(levels, k // 32))).repeat(32)
    a = np.empty((k // 512, 16))
    for p in range(k // 512):
        a[p, :8] = np.random.permutation(np.resize(levels, 8))
        for g in range(8):
            far = levels[np.abs(levels - a[p, g]) >= 10]
            a[p, g + 8] = far[np.random.randint(len(far))]
    return np.exp2(a.ravel()).repeat(32)


def f64(x):
    return np.asarray(x).astype(np.float64)


def striped(idx):
    return np.tile(idx.reshape(-1, 16).T, (8, 1)).astype(np.uint16)


def unstriped(offs):
    return offs[:16].T.reshape(-1).astype(np.int64)


E2M1 = np.array([0.0, 0.5, 1.0, 1.5, 2.0, 3.0, 4.0, 6.0, -0.0, -0.5, -1.0, -1.5, -2.0, -3.0, -4.0, -6.0])


def pack_weight(w, fmt):
    k, n = w.shape
    w = f64(np.asarray(w, np.float32).astype(ml_dtypes.bfloat16)).reshape(k // 32, 32, n)
    amax = np.abs(w).max(1)
    if fmt == "e4m3":
        byte = np.frexp(amax)[1] - 1 + 127 - 7
    else:
        mant, ex = np.frexp(amax / 6.0)
        byte = np.where(mant > 0.5, ex, ex - 1) + 127
    byte = np.clip(np.where(amax > 0, byte, 1), 1, 254)
    scaled = (w * np.exp2(127.0 - byte)[:, None, :]).reshape(k, n).astype(np.float32)
    by_word = np.ascontiguousarray(scaled.reshape(k // 512, 128, 4, n).transpose(0, 1, 3, 2))
    if fmt == "e4m3":
        words = by_word.astype(ml_dtypes.float8_e4m3fn).view(np.uint8)
    else:
        c = by_word.astype(ml_dtypes.float4_e2m1fn).view(np.uint8) & 0xF
        words = (c[..., 0::2] | (c[..., 1::2] << 4)).reshape(k // 512, 128, 2 * n)
    return np.ascontiguousarray(words), np.ascontiguousarray(byte.astype(np.uint8).reshape(k // 512, 16, n))


def unpack_weight(words, scales, fmt):
    g, _, n = scales.shape
    words = np.ascontiguousarray(words).reshape(g, 128, n, -1)
    if fmt == "e4m3":
        vals = words.view(ml_dtypes.float8_e4m3fn).astype(np.float64)
    else:
        nib = np.empty((g, 128, n, 4), np.uint8)
        nib[..., 0::2] = words & 0xF
        nib[..., 1::2] = words >> 4
        vals = E2M1[nib]
    vals = vals * np.repeat(np.exp2(scales.astype(np.float64) - 127.0), 8, axis=1)[..., None]
    return vals.transpose(0, 1, 3, 2).reshape(g * 512, n)


def gelu(v):
    return 0.5 * v * (1.0 + np.tanh(np.sqrt(2.0 / np.pi) * (v + 0.044715 * v**3)))


K, T, S, H, P, N = 512, 4096, 1024, 1024, 512, 384

def setup_inputs():
    n = np.random.standard_normal
    s = mx_kscale(K)[:, None]
    u = mx_kscale(H)[:, None]
    d = {}
    d["tab_words"], d["tab_scales"] = pack_weight(n((K, T)) * s, "e2m1")
    d["offs"] = striped(np.random.permutation(T)[:S])
    d["pos1"] = striped(np.random.permutation(S)[:P])
    d["pos2"] = striped(np.random.permutation(S)[:P])
    d["w1"] = (n((K, H)) / K ** 0.5 / s * u.T).astype(np.float32)
    d["w2"] = (n((K, H)) / K ** 0.5 / s * u.T).astype(np.float32)
    d["w3_words"], d["w3_scales"] = pack_weight(0.8 * n((K, H)) / K ** 0.5 / s * u.T, "e4m3")
    d["w4_words"], d["w4_scales"] = pack_weight(1.2 * n((H, N)) / H ** 0.5 / u, "e2m1")
    d["b4"] = (0.7 * n(N)).astype(np.float32)
    return d

def reference(tab_words, tab_scales, offs, pos1, pos2, w1, w2, w3_words, w3_scales, w4_words, w4_scales, b4):
    v = unpack_weight(tab_words, tab_scales, "e2m1")[:, unstriped(offs)]
    w3 = unpack_weight(w3_words, w3_scales, "e4m3")
    w4 = unpack_weight(w4_words, w4_scales, "e2m1")
    ra = mxq(f64(w1), 0, "e4m3").T @ v
    rb = mxq(f64(w2), 0, "e4m3").T @ v
    rd = w3.T @ v
    h = np.maximum(ra, rb) - rd
    x = np.minimum(h[:, unstriped(pos1)], h[:, unstriped(pos2)])
    y = w4.T @ mxq(x, 0, "e4m3")
    return np.exp(-np.abs(y + f64(b4)[:, None]))

@@ -1,0 +1,280 @@
+from contextlib import ExitStack
+
+import concourse.mybir as mybir
+
+K, T, S, H, PAIRS, N = 512, 4096, 1024, 1024, 512, 384
+FLOPS = 3 * 2 * K * H * S + 2 * H * N * PAIRS
+
+F32 = mybir.dt.float32
+BF16 = mybir.dt.bfloat16
+I32 = mybir.dt.int32
+U32 = mybir.dt.uint32
+U16 = mybir.dt.uint16
+U8 = mybir.dt.uint8
+FP8X4 = mybir.dt.float8_e4m3fn_x4
+FP4X4 = mybir.dt.float4_e2m1fn_x4
+ALU = mybir.AluOpType
+ACT = mybir.ActivationFunctionType
+
+P = 128
+PASS = 512
+BANK = 512
+PARTS = ((0, 384), (384, PAIRS))
+
+
+def tile_list_earring_closeness_kernel(
+    tc, tab_words, tab_scales, offs, pos1, pos2, w1, w2, w3_words, w3_scales, w4_words, w4_scales, b4, out
+):
+    nc = tc.nc
+    with ExitStack() as ctx:
+        keep = ctx.enter_context(tc.tile_pool(name="keep", bufs=1))
+        ring = ctx.enter_context(tc.tile_pool(name="ring", bufs=2))
+        psum = ctx.enter_context(tc.psum_pool(name="psum", bufs=1))
+
+        offs_t = keep.tile([P, S // 16], U16, name="offs_t")
+        pos1_t = keep.tile([P, PAIRS // 16], U16, name="pos1_t")
+        pos2_t = keep.tile([P, PAIRS // 16], U16, name="pos2_t")
+        tab_w = keep.tile([P, T], U16, name="tab_w", align_bytes=64)
+        tab_s = ring.tile([P, T], U8, name="tab_s", tag="planes", bufs=1, align_bytes=64)
+        v_w = keep.tile([P, S], U16, name="v_w", align_bytes=64)
+        v_s = keep.tile([P, S], U8, name="v_s", align_bytes=64)
+        w3_s_raw = ring.tile([P, H], U8, name="w3_s_raw", tag="rows", bufs=1, align_bytes=64)
+        bias = keep.tile([P, N // P], F32, name="bias")
+
+        nc.vector.memset(tab_s[:].bitcast(I32), 0)
+        nc.gpsimd.memset(w3_s_raw[:].bitcast(I32), 0)
+
+        warm = keep.tile([P, 2], F32, name="warm")
+        nc.gpsimd.memset(warm[:, 0:1], 0.0)
+        nc.scalar.activation(warm[:, 1:2], warm[:, 0:1], ACT.Exp)
+        nc.sync.dma_start(offs_t[:], offs)
+        nc.sync.dma_start(pos1_t[:], pos1)
+        nc.sync.dma_start(pos2_t[:], pos2)
+        nc.sync.dma_start(tab_w[:].bitcast(I32), tab_words[0].bitcast(I32))
+        for q in range(4):
+            nc.scalar.dma_start(
+                tab_s[32 * q : 32 * q + 4, :].bitcast(I32), tab_scales[0, 4 * q : 4 * q + 4, :].bitcast(I32)
+            )
+        for q in range(4):
+            nc.gpsimd.dma_start(
+                w3_s_raw[32 * q : 32 * q + 4, :].bitcast(I32), w3_scales[0, 4 * q : 4 * q + 4, :].bitcast(I32)
+            )
+
+        def load_half(w, b):
+            raw = ring.tile([P, 4, PASS], F32, name="raw", tag="raw", bufs=2)
+            nc.sync.dma_start(raw[:], w[:, b * PASS : (b + 1) * PASS].rearrange("(p j) c -> p j c", j=4))
+            return raw
+
+        raws = {}
+        raws[0, 0] = load_half(w1, 0)
+        raws[1, 0] = load_half(w2, 0)
+        w3_w_raw = ring.tile([P, H], I32, name="w3_w_raw", tag="words", bufs=1, align_bytes=64)
+        nc.sync.dma_start(w3_w_raw[:], w3_words[0].rearrange("p c i -> p (c i)").bitcast(I32))
+
+        with nc.allow_non_contiguous_dma(reason="one bias value for each partition"):
+            nc.gpsimd.dma_start(bias[:], b4.rearrange("(c p) -> p c", p=P))
+
+        nc.vector.tensor_copy(v_w[:], tab_w[:].indirect(offs_t[:]))
+        nc.vector.tensor_copy(v_s[:], tab_s[:].indirect(offs_t[:]))
+
+        grouped, codes, scales = {}, {}, {}
+        for i in range(2):
+            for b in range(2):
+                for u in range(2):
+                    grouped[i, b, u] = keep.tile([P, 2, P, 4], BF16, name="grouped_%d_%d_%d" % (i, b, u), align_bytes=64)
+                    codes[i, b, u] = keep.tile([P, 2 * P], U32, name="codes_%d_%d_%d" % (i, b, u), align_bytes=64)
+                    scales[i, b, u] = keep.tile([P, 2 * P], U8, name="scales_%d_%d_%d" % (i, b, u), align_bytes=64)
+
+        def interleave(i, b, u, on_vector):
+            src = raws[i, b][:].rearrange("p j (m t) -> p m j t", t=4)[:, :, :, 2 * u : 2 * u + 2]
+            dst = grouped[i, b, u][:].rearrange("p e m j -> p m j e")
+            if on_vector:
+                nc.vector.tensor_copy(dst, src)
+            else:
+                nc.scalar.copy(dst, src)
+
+        def quantise(i, b, u):
+            nc.vector.quantize_mx(
+                out=codes[i, b, u][:].bitcast(FP8X4),
+                scales=scales[i, b, u][:],
+                in_=grouped[i, b, u][:].rearrange("p e m j -> p (e m j)"),
+            )
+
+        w3_w = keep.tile([P, H], I32, name="w3_w", align_bytes=64)
+        w3_s = ring.tile([P, H], U8, name="w3_s", tag="planes", bufs=1, align_bytes=64)
+
+        interleave(0, 0, 0, False)
+        interleave(0, 0, 1, False)
+        interleave(1, 0, 0, True)
+        quantise(0, 0, 0)
+        nc.vector.tensor_copy(
+            w3_s[:].rearrange("p (b t m) -> p b t m", b=2, t=4), w3_s_raw[:].rearrange("p (b m t) -> p b t m", b=2, t=4)
+        )
+        quantise(1, 0, 0)
+        nc.vector.tensor_copy(
+            w3_w[:].rearrange("p (b t m) -> p b m t", b=2, t=4), w3_w_raw[:].rearrange("p (b m t) -> p b m t", b=2, t=4)
+        )
+        interleave(1, 0, 1, True)
+        quantise(0, 0, 1)
+        raws[0, 1] = load_half(w1, 1)
+        raws[1, 1] = load_half(w2, 1)
+        w4_w = ring.tile([P, 2, 2 * N], U8, name="w4_w", tag="words", bufs=1, align_bytes=64)
+        nc.sync.dma_start(w4_w[:].bitcast(I32), w4_words.rearrange("a p c -> p a c").bitcast(I32))
+
+        w4_s = ring.tile([P, 2, N], U8, name="w4_s", tag="rows", bufs=1, align_bytes=64)
+        nc.gpsimd.memset(w4_s[:].bitcast(I32), 0)
+        for q in range(4):
+            nc.sync.dma_start(
+                w4_s[32 * q : 32 * q + 4, :, :].bitcast(I32),
+                w4_scales[:, 4 * q : 4 * q + 4, :].rearrange("a r n -> r a n").bitcast(I32),
+            )
+
+        h = [keep.tile([P, S], F32, name="h_%d" % r) for r in range(H // P)]
+        held = {}
+
+        def products(r, half):
+            b, t = divmod(r, 4)
+            u, e = divmod(t, 2)
+            cols = slice(half * BANK, (half + 1) * BANK)
+            banks = []
+            for tag, bufs, lhs, lhs_scale in (
+                ("ra", 2, codes[0, b, u][:, e * P : (e + 1) * P], scales[0, b, u][:, e * P : (e + 1) * P]),
+                ("rb", 3, codes[1, b, u][:, e * P : (e + 1) * P], scales[1, b, u][:, e * P : (e + 1) * P]),
+                ("rd", 3, w3_w[:, r * P : (r + 1) * P], w3_s[:, r * P : (r + 1) * P]),
+            ):
+                bank = psum.tile([P, BANK], F32, name=tag, tag=tag, bufs=bufs)
+                nc.tensor.matmul_mx(
+                    out=bank[:],
+                    lhsT=lhs.bitcast(FP8X4),
+                    lhsT_scale=lhs_scale,
+                    rhs=v_w[:, cols].bitcast(FP4X4),
+                    rhs_scale=v_s[:, cols],
+                    start=True,
+                    stop=True,
+                )
+                banks.append(bank)
+            ra_sb = ring.tile([P, BANK], F32, name="ra_sb", tag="ra_sb", bufs=3)
+            nc.scalar.copy(ra_sb[:], banks[0][:])
+            rd_sb = ring.tile([P, BANK], F32, name="rd_sb", tag="rd_sb", bufs=3)
+            nc.scalar.copy(rd_sb[:], banks[2][:])
+            held[r, half] = (ra_sb, banks[1], rd_sb)
+
+        larger = {}
+
+        def take_max(r, half):
+            ra_sb, rb, rd = held[r, half]
+            m = ring.tile([P, BANK], F32, name="m", tag="m", bufs=3)
+            nc.vector.tensor_tensor(m[:], rb[:], ra_sb[:], ALU.max)
+            larger[r, half] = m
+
+        def subtract(r, half):
+            rd = held[r, half][2]
+            nc.gpsimd.tensor_tensor(h[r][:, half * BANK : (half + 1) * BANK], larger[r, half][:], rd[:], ALU.subtract)
+
+        chunks = {0: ((0, PAIRS),), 1: PARTS}
+        picked, x_codes, x_scales = {}, {}, {}
+        for b in range(2):
+            for j0, j1 in chunks[b]:
+                x_codes[b, j0] = keep.tile([P, j1 - j0], U32, name="x_codes_%d_%d" % (b, j0), align_bytes=64)
+                x_scales[b, j0] = keep.tile([P, j1 - j0], U8, name="x_scales_%d_%d" % (b, j0), align_bytes=64)
+
+        def gather(r, side, j0, j1):
+            b, t = divmod(r, 4)
+            pos_t = (pos1_t, pos2_t)[side]
+            if t == 0:
+                picked[b, j0, side] = ring.tile(
+                    [P, 4, j1 - j0], F32, name="picked", tag="picked_%d_%d" % (b, side), bufs=1
+                )
+            nc.vector.tensor_copy(picked[b, j0, side][:, t, :], h[r][:].indirect(pos_t[:, j0 // 16 : j1 // 16]))
+
+        x_bf = {}
+
+        def pair_min(b, j0, j1):
+            x_bf[b, j0] = keep.tile([P, j1 - j0, 4], BF16, name="x_bf_%d_%d" % (b, j0), align_bytes=64)
+            nc.vector.tensor_tensor(
+                x_bf[b, j0][:].rearrange("p (c i) t -> p c t i", i=2),
+                picked[b, j0, 0][:].rearrange("p t (c i) -> p c t i", i=2),
+                picked[b, j0, 1][:].rearrange("p t (c i) -> p c t i", i=2),
+                ALU.min,
+            )
+
+        def quantise_x(b, j0, j1):
+            done = 0
+            for width in (512, 256, 128):
+                if (j1 - j0) & width:
+                    nc.vector.quantize_mx(
+                        out=x_codes[b, j0][:, done : done + width].bitcast(FP8X4),
+                        scales=x_scales[b, j0][:, done : done + width],
+                        in_=x_bf[b, j0][:, done : done + width, :].rearrange("p j t -> p (j t)"),
+                    )
+                    done = done + width
+
+        def second_product(y, nt, j0, c0):
+            for a in range(2):
+                first = 0 if a == 0 else j0
+                cols = slice(c0 - first, c0 - first + P)
+                nc.tensor.matmul_mx(
+                    out=y,
+                    lhsT=w4_w[:, a, 2 * nt * P : 2 * (nt + 1) * P].bitcast(FP4X4),
+                    lhsT_scale=w4_s[:, a, nt * P : (nt + 1) * P],
+                    rhs=x_codes[a, first][:, cols].bitcast(FP8X4),
+                    rhs_scale=x_scales[a, first][:, cols],
+                    start=(a == 0),
+                    stop=(a == 1),
+                )
+
+        out_v = out.rearrange("(a p) j -> p a j", p=P)
+
+        def finish(j0, j1):
+            width = j1 - j0
+            dist = keep.tile([P, N // P, width], F32, name="dist_%d" % j0)
+            close = keep.tile([P, N // P, width], F32, name="close_%d" % j0)
+            for nt, (tag, bufs) in enumerate((("ra", 2), ("rb", 3), ("rd", 3))):
+                y = psum.tile([P, BANK], F32, name=tag, tag=tag, bufs=bufs)
+                for c0 in range(j0, j1, P):
+                    second_product(y[:, c0 - j0 : c0 - j0 + P], nt, j0, c0)
+                nc.scalar.activation(dist[:, nt, :], y[:, 0:width], ACT.Abs, bias=bias[:, nt : nt + 1])
+            nc.scalar.activation(close[:], dist[:], ACT.Exp, scale=-1.0)
+            nc.sync.dma_start(out_v[:, :, j0:j1], close[:])
+
+        rows = H // P
+        products(0, 0)
+        quantise(1, 0, 1)
+        products(0, 1)
+        take_max(0, 0)
+        take_max(0, 1)
+        for r in range(rows):
+            b = r // 4
+            j0, j1 = chunks[b][0]
+            subtract(r, 0)
+            subtract(r, 1)
+            if r + 1 < rows:
+                products(r + 1, 0)
+                products(r + 1, 1)
+                take_max(r + 1, 0)
+            if r in (0, 1):
+                interleave(r, 1, 0, False)
+                interleave(r, 1, 1, False)
+            gather(r, 0, j0, j1)
+            if r + 1 < rows:
+                take_max(r + 1, 1)
+            gather(r, 1, j0, j1)
+            if r in (1, 2):
+                quantise(r - 1, 1, 0)
+                quantise(r - 1, 1, 1)
+            if r == 4:
+                pair_min(0, 0, PAIRS)
+            if r == 5:
+                quantise_x(0, 0, PAIRS)
+        (j0, j1), (k0, k1) = PARTS
+        pair_min(1, j0, j1)
+        gather(4, 0, k0, k1)
+        quantise_x(1, j0, j1)
+        gather(4, 1, k0, k1)
+        finish(j0, j1)
+        for r in range(5, rows):
+            gather(r, 0, k0, k1)
+            gather(r, 1, k0, k1)
+        pair_min(1, k0, k1)
+        quantise_x(1, k0, k1)
+        finish(k0, k1)

@@ -44,9 +44,6 @@ def tile_list_earring_closeness_kernel(
         nc.vector.memset(tab_s[:].bitcast(I32), 0)
         nc.gpsimd.memset(w3_s_raw[:].bitcast(I32), 0)
 
-        warm = keep.tile([P, 2], F32, name="warm")
-        nc.gpsimd.memset(warm[:, 0:1], 0.0)
-        nc.scalar.activation(warm[:, 1:2], warm[:, 0:1], ACT.Exp)
         nc.sync.dma_start(offs_t[:], offs)
         nc.sync.dma_start(pos1_t[:], pos1)
         nc.sync.dma_start(pos2_t[:], pos2)
@@ -105,7 +102,7 @@ def tile_list_earring_closeness_kernel(
 
         interleave(0, 0, 0, False)
         interleave(0, 0, 1, False)
-        interleave(1, 0, 0, True)
+        interleave(1, 0, 0, False)
         quantise(0, 0, 0)
         nc.vector.tensor_copy(
             w3_s[:].rearrange("p (b t m) -> p b t m", b=2, t=4), w3_s_raw[:].rearrange("p (b m t) -> p b t m", b=2, t=4)
@@ -114,7 +111,7 @@ def tile_list_earring_closeness_kernel(
         nc.vector.tensor_copy(
             w3_w[:].rearrange("p (b t m) -> p b m t", b=2, t=4), w3_w_raw[:].rearrange("p (b m t) -> p b m t", b=2, t=4)
         )
-        interleave(1, 0, 1, True)
+        interleave(1, 0, 1, False)
         quantise(0, 0, 1)
         raws[0, 1] = load_half(w1, 1)
         raws[1, 1] = load_half(w2, 1)
@@ -155,9 +152,7 @@ def tile_list_earring_closeness_kernel(
                 banks.append(bank)
             ra_sb = ring.tile([P, BANK], F32, name="ra_sb", tag="ra_sb", bufs=3)
             nc.scalar.copy(ra_sb[:], banks[0][:])
-            rd_sb = ring.tile([P, BANK], F32, name="rd_sb", tag="rd_sb", bufs=3)
-            nc.scalar.copy(rd_sb[:], banks[2][:])
-            held[r, half] = (ra_sb, banks[1], rd_sb)
+            held[r, half] = (ra_sb, banks[1], banks[2])
 
         larger = {}
 
@@ -169,7 +164,7 @@ def tile_list_earring_closeness_kernel(
 
         def subtract(r, half):
             rd = held[r, half][2]
-            nc.gpsimd.tensor_tensor(h[r][:, half * BANK : (half + 1) * BANK], larger[r, half][:], rd[:], ALU.subtract)
+            nc.vector.tensor_tensor(h[r][:, half * BANK : (half + 1) * BANK], larger[r, half][:], rd[:], ALU.subtract)
 
         chunks = {0: ((0, PAIRS),), 1: PARTS}
         picked, x_codes, x_scales = {}, {}, {}
@@ -209,33 +204,38 @@ def tile_list_earring_closeness_kernel(
                     )
                     done = done + width
 
-        def second_product(y, nt, j0, c0):
-            for a in range(2):
-                first = 0 if a == 0 else j0
+        y = {}
+
+        def second_product(a, j0, j1):
+            first = 0 if a == 0 else j0
+            for c0 in range(j0, j1, P):
+                if a == 0:
+                    tag, bufs = (("ra", 2), ("rb", 3), ("rd", 3), ("ra", 2))[c0 // P]
+                    y[c0] = psum.tile([P, BANK], F32, name=tag, tag=tag, bufs=bufs)
                 cols = slice(c0 - first, c0 - first + P)
-                nc.tensor.matmul_mx(
-                    out=y,
-                    lhsT=w4_w[:, a, 2 * nt * P : 2 * (nt + 1) * P].bitcast(FP4X4),
-                    lhsT_scale=w4_s[:, a, nt * P : (nt + 1) * P],
-                    rhs=x_codes[a, first][:, cols].bitcast(FP8X4),
-                    rhs_scale=x_scales[a, first][:, cols],
-                    start=(a == 0),
-                    stop=(a == 1),
-                )
+                for nt in range(N // P):
+                    nc.tensor.matmul_mx(
+                        out=y[c0][:, nt * P : (nt + 1) * P],
+                        lhsT=w4_w[:, a, 2 * nt * P : 2 * (nt + 1) * P].bitcast(FP4X4),
+                        lhsT_scale=w4_s[:, a, nt * P : (nt + 1) * P],
+                        rhs=x_codes[a, first][:, cols].bitcast(FP8X4),
+                        rhs_scale=x_scales[a, first][:, cols],
+                        start=(a == 0 and nt == 0),
+                        stop=(a == 1 and nt == N // P - 1),
+                    )
 
         out_v = out.rearrange("(a p) j -> p a j", p=P)
 
         def finish(j0, j1):
-            width = j1 - j0
-            dist = keep.tile([P, N // P, width], F32, name="dist_%d" % j0)
-            close = keep.tile([P, N // P, width], F32, name="close_%d" % j0)
-            for nt, (tag, bufs) in enumerate((("ra", 2), ("rb", 3), ("rd", 3))):
-                y = psum.tile([P, BANK], F32, name=tag, tag=tag, bufs=bufs)
-                for c0 in range(j0, j1, P):
-                    second_product(y[:, c0 - j0 : c0 - j0 + P], nt, j0, c0)
-                nc.scalar.activation(dist[:, nt, :], y[:, 0:width], ACT.Abs, bias=bias[:, nt : nt + 1])
-            nc.scalar.activation(close[:], dist[:], ACT.Exp, scale=-1.0)
-            nc.sync.dma_start(out_v[:, :, j0:j1], close[:])
+            for c0 in range(j0, j1, P):
+                dist = keep.tile([P, N // P, P], F32, name="dist_%d" % c0)
+                close = keep.tile([P, N // P, P], F32, name="close_%d" % c0)
+                for nt in range(N // P):
+                    nc.scalar.activation(
+                        dist[:, nt, :], y[c0][:, nt * P : (nt + 1) * P], ACT.Abs, bias=bias[:, nt : nt + 1]
+                    )
+                nc.scalar.activation(close[:], dist[:], ACT.Exp, scale=-1.0)
+                nc.sync.dma_start(out_v[:, :, c0 : c0 + P], close[:])
 
         rows = H // P
         products(0, 0)
@@ -267,14 +267,17 @@ def tile_list_earring_closeness_kernel(
             if r == 5:
                 quantise_x(0, 0, PAIRS)
         (j0, j1), (k0, k1) = PARTS
+        second_product(0, 0, PAIRS)
         pair_min(1, j0, j1)
         gather(4, 0, k0, k1)
         quantise_x(1, j0, j1)
         gather(4, 1, k0, k1)
+        second_product(1, j0, j1)
         finish(j0, j1)
         for r in range(5, rows):
             gather(r, 0, k0, k1)
             gather(r, 1, k0, k1)
         pair_min(1, k0, k1)
         quantise_x(1, k0, k1)
+        second_product(1, k0, k1)
         finish(k0, k1)

@@ -1,6 +1,7 @@
 from contextlib import ExitStack
 
 import concourse.mybir as mybir
+from concourse.masks import make_identity
 
 K, T, S, H, PAIRS, N = 512, 4096, 1024, 1024, 512, 384
 FLOPS = 3 * 2 * K * H * S + 2 * H * N * PAIRS
@@ -45,6 +46,7 @@ def tile_list_earring_closeness_kernel(
         nc.gpsimd.memset(w3_s_raw[:].bitcast(I32), 0)
 
         nc.sync.dma_start(offs_t[:], offs)
+        ident = keep.tile([P, P], F32, name="ident")
         nc.sync.dma_start(pos1_t[:], pos1)
         nc.sync.dma_start(pos2_t[:], pos2)
         nc.sync.dma_start(tab_w[:].bitcast(I32), tab_words[0].bitcast(I32))
@@ -71,6 +73,7 @@ def tile_list_earring_closeness_kernel(
         with nc.allow_non_contiguous_dma(reason="one bias value for each partition"):
             nc.gpsimd.dma_start(bias[:], b4.rearrange("(c p) -> p c", p=P))
 
+        make_identity(nc, ident[:])
         nc.vector.tensor_copy(v_w[:], tab_w[:].indirect(offs_t[:]))
         nc.vector.tensor_copy(v_s[:], tab_s[:].indirect(offs_t[:]))
 
@@ -136,8 +139,8 @@ def tile_list_earring_closeness_kernel(
             banks = []
             for tag, bufs, lhs, lhs_scale in (
                 ("ra", 2, codes[0, b, u][:, e * P : (e + 1) * P], scales[0, b, u][:, e * P : (e + 1) * P]),
-                ("rb", 3, codes[1, b, u][:, e * P : (e + 1) * P], scales[1, b, u][:, e * P : (e + 1) * P]),
-                ("rd", 3, w3_w[:, r * P : (r + 1) * P], w3_s[:, r * P : (r + 1) * P]),
+                ("rb", 2, codes[1, b, u][:, e * P : (e + 1) * P], scales[1, b, u][:, e * P : (e + 1) * P]),
+                ("rd", 2, w3_w[:, r * P : (r + 1) * P], w3_s[:, r * P : (r + 1) * P]),
             ):
                 bank = psum.tile([P, BANK], F32, name=tag, tag=tag, bufs=bufs)
                 nc.tensor.matmul_mx(
@@ -158,13 +161,73 @@ def tile_list_earring_closeness_kernel(
 
         def take_max(r, half):
             ra_sb, rb, rd = held[r, half]
-            m = ring.tile([P, BANK], F32, name="m", tag="m", bufs=3)
+            m = ring.tile([P, BANK], F32, name="m", tag="m", bufs=4)
             nc.vector.tensor_tensor(m[:], rb[:], ra_sb[:], ALU.max)
             larger[r, half] = m
 
         def subtract(r, half):
             rd = held[r, half][2]
             nc.vector.tensor_tensor(h[r][:, half * BANK : (half + 1) * BANK], larger[r, half][:], rd[:], ALU.subtract)
+
+        turned = {}
+
+        def turned_products(g, k):
+            b, u = divmod(g, 2)
+            pair = slice(g * 2 * P, (g + 1) * 2 * P)
+            banks = []
+            for tag, rhs, rhs_scale in (
+                ("ra", codes[0, b, u][:], scales[0, b, u][:]),
+                ("rb", codes[1, b, u][:], scales[1, b, u][:]),
+                ("rd", w3_w[:, pair], w3_s[:, pair]),
+            ):
+                bank = psum.tile([P, BANK], F32, name=tag, tag=tag, bufs=2)
+                for i in range(2):
+                    stones = slice((2 * k + i) * P, (2 * k + i + 1) * P)
+                    nc.tensor.matmul_mx(
+                        out=bank[:, i * 2 * P : (i + 1) * 2 * P],
+                        lhsT=v_w[:, stones].bitcast(FP4X4),
+                        lhsT_scale=v_s[:, stones],
+                        rhs=rhs.bitcast(FP8X4),
+                        rhs_scale=rhs_scale,
+                        start=True,
+                        stop=True,
+                    )
+                banks.append(bank)
+            if k % 2 == 0:
+                ra_tile = ring.tile([P, BANK], F32, name="ra_sb", tag="ra_sb", bufs=3)
+                ra_sb = ra_tile[:]
+            else:
+                pb, pu = divmod(g - 1, 2)
+                j0, j1 = chunks[pb][0]
+                middle = (2 * pu + 1) * (j1 - j0)
+                ra_sb = picked_tile(pb, k // 2, j0, j1)[:, middle - BANK // 2 : middle + BANK // 2]
+            nc.scalar.copy(ra_sb, banks[0][:])
+            neg_rd = ring.tile([P, BANK], F32, name="neg_rd", tag="neg_rd", bufs=4)
+            nc.scalar.activation(neg_rd[:], banks[2][:], ACT.Copy, scale=-1.0)
+            turned[g, k] = (ra_sb, banks[1], neg_rd)
+
+        def turned_max(g, k):
+            ra_sb, rb, neg_rd = turned[g, k]
+            m = ring.tile([P, BANK], F32, name="m", tag="m", bufs=4)
+            nc.vector.tensor_tensor(m[:], rb[:], ra_sb, ALU.max)
+            turned[g, k] = (m, neg_rd)
+
+        def turn_back(g, half):
+            for e in range(2):
+                bank = psum.tile([P, BANK], F32, name="hb", tag="hb", bufs=2)
+                for i in range(4):
+                    k, within = divmod(4 * half + i, 2)
+                    cols = slice((2 * within + e) * P, (2 * within + e + 1) * P)
+                    for first, src in ((True, turned[g, k][1]), (False, turned[g, k][0])):
+                        nc.tensor.matmul(
+                            bank[:, i * P : (i + 1) * P],
+                            src[:, cols],
+                            ident[:],
+                            start=first,
+                            stop=not first,
+                            is_transpose=True,
+                        )
+                nc.scalar.copy(h[2 * g + e][:, half * BANK : (half + 1) * BANK], bank[:])
 
         chunks = {0: ((0, PAIRS),), 1: PARTS}
         picked, x_codes, x_scales = {}, {}, {}
@@ -173,14 +236,18 @@ def tile_list_earring_closeness_kernel(
                 x_codes[b, j0] = keep.tile([P, j1 - j0], U32, name="x_codes_%d_%d" % (b, j0), align_bytes=64)
                 x_scales[b, j0] = keep.tile([P, j1 - j0], U8, name="x_scales_%d_%d" % (b, j0), align_bytes=64)
 
+        def picked_tile(b, side, j0, j1):
+            if (b, j0, side) not in picked:
+                picked[b, j0, side] = ring.tile(
+                    [P, 4 * (j1 - j0)], F32, name="picked", tag="picked_%d_%d" % (b, side), bufs=1
+                )
+            return picked[b, j0, side]
+
         def gather(r, side, j0, j1):
             b, t = divmod(r, 4)
             pos_t = (pos1_t, pos2_t)[side]
-            if t == 0:
-                picked[b, j0, side] = ring.tile(
-                    [P, 4, j1 - j0], F32, name="picked", tag="picked_%d_%d" % (b, side), bufs=1
-                )
-            nc.vector.tensor_copy(picked[b, j0, side][:, t, :], h[r][:].indirect(pos_t[:, j0 // 16 : j1 // 16]))
+            width = j1 - j0
+            nc.vector.tensor_copy(picked_tile(b, side, j0, j1)[:, t * width : (t + 1) * width], h[r][:].indirect(pos_t[:, j0 // 16 : j1 // 16]))
 
         x_bf = {}
 
@@ -188,8 +255,8 @@ def tile_list_earring_closeness_kernel(
             x_bf[b, j0] = keep.tile([P, j1 - j0, 4], BF16, name="x_bf_%d_%d" % (b, j0), align_bytes=64)
             nc.vector.tensor_tensor(
                 x_bf[b, j0][:].rearrange("p (c i) t -> p c t i", i=2),
-                picked[b, j0, 0][:].rearrange("p t (c i) -> p c t i", i=2),
-                picked[b, j0, 1][:].rearrange("p t (c i) -> p c t i", i=2),
+                picked[b, j0, 0][:].rearrange("p (t c i) -> p c t i", t=4, i=2),
+                picked[b, j0, 1][:].rearrange("p (t c i) -> p c t i", t=4, i=2),
                 ALU.min,
             )
 
@@ -210,7 +277,7 @@ def tile_list_earring_closeness_kernel(
             first = 0 if a == 0 else j0
             for c0 in range(j0, j1, P):
                 if a == 0:
-                    tag, bufs = (("ra", 2), ("rb", 3), ("rd", 3), ("ra", 2))[c0 // P]
+                    tag, bufs = (("ra", 2), ("rb", 2), ("rd", 2), ("ra", 2))[c0 // P]
                     y[c0] = psum.tile([P, BANK], F32, name=tag, tag=tag, bufs=bufs)
                 cols = slice(c0 - first, c0 - first + P)
                 for nt in range(N // P):
@@ -238,33 +305,33 @@ def tile_list_earring_closeness_kernel(
                 nc.sync.dma_start(out_v[:, :, c0 : c0 + P], close[:])
 
         rows = H // P
-        products(0, 0)
-        quantise(1, 0, 1)
-        products(0, 1)
-        take_max(0, 0)
-        take_max(0, 1)
-        for r in range(rows):
-            b = r // 4
+        for r in range(2):
+            for half in range(2):
+                products(r, half)
+            if r == 0:
+                quantise(1, 0, 1)
+            for half in range(2):
+                take_max(r, half)
+            for half in range(2):
+                subtract(r, half)
+        for g in range(4):
+            b = g // 2
             j0, j1 = chunks[b][0]
-            subtract(r, 0)
-            subtract(r, 1)
-            if r + 1 < rows:
-                products(r + 1, 0)
-                products(r + 1, 1)
-                take_max(r + 1, 0)
-            if r in (0, 1):
-                interleave(r, 1, 0, False)
-                interleave(r, 1, 1, False)
-            gather(r, 0, j0, j1)
-            if r + 1 < rows:
-                take_max(r + 1, 1)
-            gather(r, 1, j0, j1)
-            if r in (1, 2):
-                quantise(r - 1, 1, 0)
-                quantise(r - 1, 1, 1)
-            if r == 4:
+            for half in range(2):
+                if g + 1 < 4:
+                    for k in (2 * half, 2 * half + 1):
+                        turned_products(g + 1, k)
+                        turned_max(g + 1, k)
+                    turn_back(g + 1, half)
+                if g < 2:
+                    interleave(half, 1, g, False)
+                gather(2 * g, half, j0, j1)
+                gather(2 * g + 1, half, j0, j1)
+                if g < 2:
+                    quantise(half, 1, g)
+            if g == 1:
                 pair_min(0, 0, PAIRS)
-            if r == 5:
+            if g == 2:
                 quantise_x(0, 0, PAIRS)
         (j0, j1), (k0, k1) = PARTS
         second_product(0, 0, PAIRS)

@@ -20,7 +20,8 @@ ACT = mybir.ActivationFunctionType
 P = 128
 PASS = 512
 BANK = 512
-PARTS = ((0, 384), (384, PAIRS))
+PARTS = ((0, 256), (256, 384), (384, PAIRS))
+PART_BASE = {0: 512, 256: 256, 384: 0}
 
 
 def tile_list_earring_closeness_kernel(
@@ -193,14 +194,14 @@ def tile_list_earring_closeness_kernel(
                         stop=True,
                     )
                 banks.append(bank)
-            if k % 2 == 0:
+            if g == 3:
+                ra_sb = picked_all[1][k // 2][:, (k % 2) * BANK : (k % 2 + 1) * BANK]
+            elif k % 2 == 0 or (g, k) == (1, 1):
                 ra_tile = ring.tile([P, BANK], F32, name="ra_sb", tag="ra_sb", bufs=3)
                 ra_sb = ra_tile[:]
             else:
-                pb, pu = divmod(g - 1, 2)
-                j0, j1 = chunks[pb][0]
-                middle = (2 * pu + 1) * (j1 - j0)
-                ra_sb = picked_tile(pb, k // 2, j0, j1)[:, middle - BANK // 2 : middle + BANK // 2]
+                middle = (2 * g - 1) * PAIRS
+                ra_sb = picked_all[0][k // 2][:, middle - BANK // 2 : middle + BANK // 2]
             nc.scalar.copy(ra_sb, banks[0][:])
             neg_rd = ring.tile([P, BANK], F32, name="neg_rd", tag="neg_rd", bufs=4)
             nc.scalar.activation(neg_rd[:], banks[2][:], ACT.Copy, scale=-1.0)
@@ -230,33 +231,38 @@ def tile_list_earring_closeness_kernel(
                 nc.scalar.copy(h[2 * g + e][:, half * BANK : (half + 1) * BANK], bank[:])
 
         chunks = {0: ((0, PAIRS),), 1: PARTS}
-        picked, x_codes, x_scales = {}, {}, {}
+        x_codes, x_scales = {}, {}
         for b in range(2):
             for j0, j1 in chunks[b]:
                 x_codes[b, j0] = keep.tile([P, j1 - j0], U32, name="x_codes_%d_%d" % (b, j0), align_bytes=64)
                 x_scales[b, j0] = keep.tile([P, j1 - j0], U8, name="x_scales_%d_%d" % (b, j0), align_bytes=64)
 
-        def picked_tile(b, side, j0, j1):
-            if (b, j0, side) not in picked:
-                picked[b, j0, side] = ring.tile(
-                    [P, 4 * (j1 - j0)], F32, name="picked", tag="picked_%d_%d" % (b, side), bufs=1
-                )
-            return picked[b, j0, side]
+        picked_all = [
+            [keep.tile([P, (4 * PAIRS, 3 * PAIRS)[b]], F32, name="picked_%d_%d" % (b, side)) for side in range(2)]
+            for b in range(2)
+        ]
+
+        def picked(b, side, j0, j1):
+            base = PART_BASE[j0] if b == 1 else 0
+            return picked_all[b][side][:, base : base + 4 * (j1 - j0)]
 
         def gather(r, side, j0, j1):
             b, t = divmod(r, 4)
             pos_t = (pos1_t, pos2_t)[side]
             width = j1 - j0
-            nc.vector.tensor_copy(picked_tile(b, side, j0, j1)[:, t * width : (t + 1) * width], h[r][:].indirect(pos_t[:, j0 // 16 : j1 // 16]))
+            nc.vector.tensor_copy(
+                picked(b, side, j0, j1)[:, t * width : (t + 1) * width],
+                h[r][:].indirect(pos_t[:, j0 // 16 : j1 // 16]),
+            )
 
         x_bf = {}
 
         def pair_min(b, j0, j1):
             x_bf[b, j0] = keep.tile([P, j1 - j0, 4], BF16, name="x_bf_%d_%d" % (b, j0), align_bytes=64)
             nc.vector.tensor_tensor(
-                x_bf[b, j0][:].rearrange("p (c i) t -> p c t i", i=2),
-                picked[b, j0, 0][:].rearrange("p (t c i) -> p c t i", t=4, i=2),
-                picked[b, j0, 1][:].rearrange("p (t c i) -> p c t i", t=4, i=2),
+                x_bf[b, j0][:].rearrange("p (c i) t -> p c t i", i=4),
+                picked(b, 0, j0, j1).rearrange("p (t c i) -> p c t i", t=4, i=4),
+                picked(b, 1, j0, j1).rearrange("p (t c i) -> p c t i", t=4, i=4),
                 ALU.min,
             )
 
@@ -272,23 +278,27 @@ def tile_list_earring_closeness_kernel(
                     done = done + width
 
         y = {}
+        y_tags = ("ra", "rb", "rd")
 
         def second_product(a, j0, j1):
             first = 0 if a == 0 else j0
             for c0 in range(j0, j1, P):
-                if a == 0:
-                    tag, bufs = (("ra", 2), ("rb", 2), ("rd", 2), ("ra", 2))[c0 // P]
-                    y[c0] = psum.tile([P, BANK], F32, name=tag, tag=tag, bufs=bufs)
+                last = c0 == PAIRS - P
                 cols = slice(c0 - first, c0 - first + P)
                 for nt in range(N // P):
+                    if a == 0 and (last or nt == 0):
+                        tag = y_tags[nt if last else c0 // P]
+                        bank = psum.tile([P, BANK], F32, name=tag, tag=tag, bufs=2)
+                    if a == 0:
+                        y[c0, nt] = bank[:, nt * P : (nt + 1) * P]
                     nc.tensor.matmul_mx(
-                        out=y[c0][:, nt * P : (nt + 1) * P],
+                        out=y[c0, nt],
                         lhsT=w4_w[:, a, 2 * nt * P : 2 * (nt + 1) * P].bitcast(FP4X4),
                         lhsT_scale=w4_s[:, a, nt * P : (nt + 1) * P],
                         rhs=x_codes[a, first][:, cols].bitcast(FP8X4),
                         rhs_scale=x_scales[a, first][:, cols],
-                        start=(a == 0 and nt == 0),
-                        stop=(a == 1 and nt == N // P - 1),
+                        start=(a == 0 and (last or nt == 0)),
+                        stop=(a == 1 and (last or nt == N // P - 1)),
                     )
 
         out_v = out.rearrange("(a p) j -> p a j", p=P)
@@ -299,12 +309,11 @@ def tile_list_earring_closeness_kernel(
                 close = keep.tile([P, N // P, P], F32, name="close_%d" % c0)
                 for nt in range(N // P):
                     nc.scalar.activation(
-                        dist[:, nt, :], y[c0][:, nt * P : (nt + 1) * P], ACT.Abs, bias=bias[:, nt : nt + 1]
+                        dist[:, nt, :], y[c0, nt], ACT.Abs, bias=bias[:, nt : nt + 1]
                     )
                 nc.scalar.activation(close[:], dist[:], ACT.Exp, scale=-1.0)
                 nc.sync.dma_start(out_v[:, :, c0 : c0 + P], close[:])
 
-        rows = H // P
         for r in range(2):
             for half in range(2):
                 products(r, half)
@@ -314,37 +323,29 @@ def tile_list_earring_closeness_kernel(
                 take_max(r, half)
             for half in range(2):
                 subtract(r, half)
-        for g in range(4):
-            b = g // 2
-            j0, j1 = chunks[b][0]
+        for g in range(3):
             for half in range(2):
-                if g + 1 < 4:
-                    for k in (2 * half, 2 * half + 1):
-                        turned_products(g + 1, k)
-                        turned_max(g + 1, k)
-                    turn_back(g + 1, half)
+                for k in (2 * half, 2 * half + 1):
+                    turned_products(g + 1, k)
+                    turned_max(g + 1, k)
+                turn_back(g + 1, half)
                 if g < 2:
-                    interleave(half, 1, g, False)
-                gather(2 * g, half, j0, j1)
-                gather(2 * g + 1, half, j0, j1)
+                    interleave(half, 1, g, (half, g) in ((1, 0),))
+                for j0, j1 in reversed(chunks[g // 2]):
+                    gather(2 * g, half, j0, j1)
+                    gather(2 * g + 1, half, j0, j1)
                 if g < 2:
                     quantise(half, 1, g)
             if g == 1:
                 pair_min(0, 0, PAIRS)
             if g == 2:
                 quantise_x(0, 0, PAIRS)
-        (j0, j1), (k0, k1) = PARTS
         second_product(0, 0, PAIRS)
-        pair_min(1, j0, j1)
-        gather(4, 0, k0, k1)
-        quantise_x(1, j0, j1)
-        gather(4, 1, k0, k1)
-        second_product(1, j0, j1)
-        finish(j0, j1)
-        for r in range(5, rows):
-            gather(r, 0, k0, k1)
-            gather(r, 1, k0, k1)
-        pair_min(1, k0, k1)
-        quantise_x(1, k0, k1)
-        second_product(1, k0, k1)
-        finish(k0, k1)
+        for j0, j1 in PARTS:
+            for side in range(2):
+                gather(6, side, j0, j1)
+                gather(7, side, j0, j1)
+            pair_min(1, j0, j1)
+            quantise_x(1, j0, j1)
+            second_product(1, j0, j1)
+            finish(j0, j1)

@@ -18,10 +18,21 @@ ALU = mybir.AluOpType
 ACT = mybir.ActivationFunctionType
 
 P = 128
-PASS = 512
+PACK = 4
+PASS = P * PACK
 BANK = 512
-PARTS = ((0, 256), (256, 384), (384, PAIRS))
+QUADS = 4
+GROUP = 2 * P
+GROUPS = H // GROUP
+N_TILES = N // P
+
+PARTS = (((0, PAIRS),), ((0, 256), (256, 384), (384, PAIRS)))
 PART_BASE = {0: 512, 256: 256, 384: 0}
+PICKED_COLS = (PACK * PAIRS, PART_BASE[0] + PACK * 256)
+
+BANK_BUFS = 2
+RA_BUFS = 3
+TURN_BUFS = 4
 
 
 def tile_list_earring_closeness_kernel(
@@ -37,11 +48,11 @@ def tile_list_earring_closeness_kernel(
         pos1_t = keep.tile([P, PAIRS // 16], U16, name="pos1_t")
         pos2_t = keep.tile([P, PAIRS // 16], U16, name="pos2_t")
         tab_w = keep.tile([P, T], U16, name="tab_w", align_bytes=64)
-        tab_s = ring.tile([P, T], U8, name="tab_s", tag="planes", bufs=1, align_bytes=64)
+        tab_s = keep.tile([P, T], U8, name="tab_s", align_bytes=64)
         v_w = keep.tile([P, S], U16, name="v_w", align_bytes=64)
         v_s = keep.tile([P, S], U8, name="v_s", align_bytes=64)
         w3_s_raw = ring.tile([P, H], U8, name="w3_s_raw", tag="rows", bufs=1, align_bytes=64)
-        bias = keep.tile([P, N // P], F32, name="bias")
+        bias = keep.tile([P, N_TILES], F32, name="bias")
 
         nc.vector.memset(tab_s[:].bitcast(I32), 0)
         nc.gpsimd.memset(w3_s_raw[:].bitcast(I32), 0)
@@ -51,23 +62,23 @@ def tile_list_earring_closeness_kernel(
         nc.sync.dma_start(pos1_t[:], pos1)
         nc.sync.dma_start(pos2_t[:], pos2)
         nc.sync.dma_start(tab_w[:].bitcast(I32), tab_words[0].bitcast(I32))
-        for q in range(4):
+        for q in range(QUADS):
             nc.scalar.dma_start(
                 tab_s[32 * q : 32 * q + 4, :].bitcast(I32), tab_scales[0, 4 * q : 4 * q + 4, :].bitcast(I32)
             )
-        for q in range(4):
+        for q in range(QUADS):
             nc.gpsimd.dma_start(
                 w3_s_raw[32 * q : 32 * q + 4, :].bitcast(I32), w3_scales[0, 4 * q : 4 * q + 4, :].bitcast(I32)
             )
 
-        def load_half(w, b):
-            raw = ring.tile([P, 4, PASS], F32, name="raw", tag="raw", bufs=2)
-            nc.sync.dma_start(raw[:], w[:, b * PASS : (b + 1) * PASS].rearrange("(p j) c -> p j c", j=4))
+        def load_columns(w, a):
+            raw = ring.tile([P, PACK, PASS], F32, name="raw", tag="raw", bufs=2)
+            nc.sync.dma_start(raw[:], w[:, a * PASS : (a + 1) * PASS].rearrange("(p i) c -> p i c", i=PACK))
             return raw
 
         raws = {}
-        raws[0, 0] = load_half(w1, 0)
-        raws[1, 0] = load_half(w2, 0)
+        raws[0, 0] = load_columns(w1, 0)
+        raws[1, 0] = load_columns(w2, 0)
         w3_w_raw = ring.tile([P, H], I32, name="w3_w_raw", tag="words", bufs=1, align_bytes=64)
         nc.sync.dma_start(w3_w_raw[:], w3_words[0].rearrange("p c i -> p (c i)").bitcast(I32))
 
@@ -79,273 +90,249 @@ def tile_list_earring_closeness_kernel(
         nc.vector.tensor_copy(v_s[:], tab_s[:].indirect(offs_t[:]))
 
         grouped, codes, scales = {}, {}, {}
-        for i in range(2):
-            for b in range(2):
-                for u in range(2):
-                    grouped[i, b, u] = keep.tile([P, 2, P, 4], BF16, name="grouped_%d_%d_%d" % (i, b, u), align_bytes=64)
-                    codes[i, b, u] = keep.tile([P, 2 * P], U32, name="codes_%d_%d_%d" % (i, b, u), align_bytes=64)
-                    scales[i, b, u] = keep.tile([P, 2 * P], U8, name="scales_%d_%d_%d" % (i, b, u), align_bytes=64)
+        for w in range(2):
+            for g in range(GROUPS):
+                grouped[w, g] = keep.tile(
+                    [P, 2, P, PACK], BF16, name="grouped", tag="grouped_%d_%d" % (w, g), align_bytes=64
+                )
+                codes[w, g] = keep.tile([P, GROUP], U32, name="codes_%d_%d" % (w, g), align_bytes=64)
+                scales[w, g] = keep.tile([P, GROUP], U8, name="scales_%d_%d" % (w, g), align_bytes=64)
 
-        def interleave(i, b, u, on_vector):
-            src = raws[i, b][:].rearrange("p j (m t) -> p m j t", t=4)[:, :, :, 2 * u : 2 * u + 2]
-            dst = grouped[i, b, u][:].rearrange("p e m j -> p m j e")
-            if on_vector:
-                nc.vector.tensor_copy(dst, src)
-            else:
-                nc.scalar.copy(dst, src)
+        def interleave(w, g):
+            a, u = divmod(g, 2)
+            src = raws[w, a][:].rearrange("p i (m t) -> p m i t", t=PACK)[:, :, :, 2 * u : 2 * u + 2]
+            nc.scalar.copy(grouped[w, g][:].rearrange("p e m i -> p m i e"), src)
 
-        def quantise(i, b, u):
+        def quantise_weight(w, g):
             nc.vector.quantize_mx(
-                out=codes[i, b, u][:].bitcast(FP8X4),
-                scales=scales[i, b, u][:],
-                in_=grouped[i, b, u][:].rearrange("p e m j -> p (e m j)"),
+                out=codes[w, g][:].bitcast(FP8X4),
+                scales=scales[w, g][:],
+                in_=grouped[w, g][:].rearrange("p e m i -> p (e m i)"),
             )
 
         w3_w = keep.tile([P, H], I32, name="w3_w", align_bytes=64)
-        w3_s = ring.tile([P, H], U8, name="w3_s", tag="planes", bufs=1, align_bytes=64)
+        interleave(0, 0)
+        interleave(0, 1)
+        interleave(1, 0)
+        quantise_weight(0, 0)
+        w3_s = keep.tile([P, H], U8, name="w3_s", tag="grouped_0_0", align_bytes=64)
+        nc.vector.tensor_copy(
+            w3_s[:].rearrange("p (a t m) -> p a t m", a=2, t=PACK),
+            w3_s_raw[:].rearrange("p (a m t) -> p a t m", a=2, t=PACK),
+        )
+        quantise_weight(1, 0)
+        nc.vector.tensor_copy(
+            w3_w[:].rearrange("p (a t m) -> p a m t", a=2, t=PACK),
+            w3_w_raw[:].rearrange("p (a m t) -> p a m t", a=2, t=PACK),
+        )
+        interleave(1, 1)
+        quantise_weight(0, 1)
 
-        interleave(0, 0, 0, False)
-        interleave(0, 0, 1, False)
-        interleave(1, 0, 0, False)
-        quantise(0, 0, 0)
-        nc.vector.tensor_copy(
-            w3_s[:].rearrange("p (b t m) -> p b t m", b=2, t=4), w3_s_raw[:].rearrange("p (b m t) -> p b t m", b=2, t=4)
-        )
-        quantise(1, 0, 0)
-        nc.vector.tensor_copy(
-            w3_w[:].rearrange("p (b t m) -> p b m t", b=2, t=4), w3_w_raw[:].rearrange("p (b m t) -> p b m t", b=2, t=4)
-        )
-        interleave(1, 0, 1, False)
-        quantise(0, 0, 1)
-        raws[0, 1] = load_half(w1, 1)
-        raws[1, 1] = load_half(w2, 1)
+        raws[0, 1] = load_columns(w1, 1)
+        raws[1, 1] = load_columns(w2, 1)
         w4_w = ring.tile([P, 2, 2 * N], U8, name="w4_w", tag="words", bufs=1, align_bytes=64)
         nc.sync.dma_start(w4_w[:].bitcast(I32), w4_words.rearrange("a p c -> p a c").bitcast(I32))
-
         w4_s = ring.tile([P, 2, N], U8, name="w4_s", tag="rows", bufs=1, align_bytes=64)
         nc.gpsimd.memset(w4_s[:].bitcast(I32), 0)
-        for q in range(4):
+        for q in range(QUADS):
             nc.sync.dma_start(
                 w4_s[32 * q : 32 * q + 4, :, :].bitcast(I32),
                 w4_scales[:, 4 * q : 4 * q + 4, :].rearrange("a r n -> r a n").bitcast(I32),
             )
 
         h = [keep.tile([P, S], F32, name="h_%d" % r) for r in range(H // P)]
-        held = {}
 
-        def products(r, half):
-            b, t = divmod(r, 4)
-            u, e = divmod(t, 2)
-            cols = slice(half * BANK, (half + 1) * BANK)
+        def readings(g, cols):
+            w3_cols = slice(g * GROUP + cols.start, g * GROUP + cols.stop)
+            return (
+                ("ra", codes[0, g][:, cols], scales[0, g][:, cols]),
+                ("rb", codes[1, g][:, cols], scales[1, g][:, cols]),
+                ("rd", w3_w[:, w3_cols], w3_s[:, w3_cols]),
+            )
+
+        def new_bank(tag):
+            return psum.tile([P, BANK], F32, name=tag, tag=tag, bufs=BANK_BUFS)
+
+        def new_ra():
+            return ring.tile([P, BANK], F32, name="ra_sb", tag="ra_sb", bufs=RA_BUFS)
+
+        def take_max(rb, ra_sb):
+            larger = ring.tile([P, BANK], F32, name="larger", tag="larger", bufs=TURN_BUFS)
+            nc.vector.tensor_tensor(larger[:], rb[:], ra_sb, ALU.max)
+            return larger
+
+        def direct_products(r, half):
+            stones = slice(half * BANK, (half + 1) * BANK)
             banks = []
-            for tag, bufs, lhs, lhs_scale in (
-                ("ra", 2, codes[0, b, u][:, e * P : (e + 1) * P], scales[0, b, u][:, e * P : (e + 1) * P]),
-                ("rb", 2, codes[1, b, u][:, e * P : (e + 1) * P], scales[1, b, u][:, e * P : (e + 1) * P]),
-                ("rd", 2, w3_w[:, r * P : (r + 1) * P], w3_s[:, r * P : (r + 1) * P]),
-            ):
-                bank = psum.tile([P, BANK], F32, name=tag, tag=tag, bufs=bufs)
+            for tag, words, scale in readings(0, slice(r * P, (r + 1) * P)):
+                bank = new_bank(tag)
                 nc.tensor.matmul_mx(
                     out=bank[:],
-                    lhsT=lhs.bitcast(FP8X4),
-                    lhsT_scale=lhs_scale,
-                    rhs=v_w[:, cols].bitcast(FP4X4),
-                    rhs_scale=v_s[:, cols],
+                    lhsT=words.bitcast(FP8X4),
+                    lhsT_scale=scale,
+                    rhs=v_w[:, stones].bitcast(FP4X4),
+                    rhs_scale=v_s[:, stones],
                     start=True,
                     stop=True,
                 )
                 banks.append(bank)
-            ra_sb = ring.tile([P, BANK], F32, name="ra_sb", tag="ra_sb", bufs=3)
+            ra_sb = new_ra()
             nc.scalar.copy(ra_sb[:], banks[0][:])
-            held[r, half] = (ra_sb, banks[1], banks[2])
+            return ra_sb[:], banks[1], banks[2]
 
-        larger = {}
+        x_codes, x_scales, x_bf = {}, {}, {}
+        for a in range(2):
+            for j0, j1 in PARTS[a]:
+                x_codes[a, j0] = keep.tile([P, j1 - j0], U32, name="x_codes_%d_%d" % (a, j0), align_bytes=64)
+                x_scales[a, j0] = keep.tile([P, j1 - j0], U8, name="x_scales_%d_%d" % (a, j0), align_bytes=64)
 
-        def take_max(r, half):
-            ra_sb, rb, rd = held[r, half]
-            m = ring.tile([P, BANK], F32, name="m", tag="m", bufs=4)
-            nc.vector.tensor_tensor(m[:], rb[:], ra_sb[:], ALU.max)
-            larger[r, half] = m
+        picked_tiles = [
+            [keep.tile([P, PICKED_COLS[a]], F32, name="picked_%d_%d" % (a, side)) for side in range(2)]
+            for a in range(2)
+        ]
 
-        def subtract(r, half):
-            rd = held[r, half][2]
-            nc.vector.tensor_tensor(h[r][:, half * BANK : (half + 1) * BANK], larger[r, half][:], rd[:], ALU.subtract)
+        def picked(a, side, j0, j1):
+            base = PART_BASE[j0] if a == 1 else 0
+            return picked_tiles[a][side][:, base : base + PACK * (j1 - j0)]
 
-        turned = {}
+        def ra_staging(g, step):
+            side = step // 2
+            if g == GROUPS - 1:
+                return picked_tiles[1][side][:, (step % 2) * BANK : (step % 2 + 1) * BANK]
+            if step % 2 == 0 or (g == 1 and side == 0):
+                ra_sb = new_ra()
+                return ra_sb[:]
+            border = (2 * (g - 1) + 1) * PAIRS
+            return picked_tiles[0][side][:, border - BANK // 2 : border + BANK // 2]
 
-        def turned_products(g, k):
-            b, u = divmod(g, 2)
-            pair = slice(g * 2 * P, (g + 1) * 2 * P)
+        def turned_step(g, step):
             banks = []
-            for tag, rhs, rhs_scale in (
-                ("ra", codes[0, b, u][:], scales[0, b, u][:]),
-                ("rb", codes[1, b, u][:], scales[1, b, u][:]),
-                ("rd", w3_w[:, pair], w3_s[:, pair]),
-            ):
-                bank = psum.tile([P, BANK], F32, name=tag, tag=tag, bufs=2)
+            for tag, words, scale in readings(g, slice(0, GROUP)):
+                bank = new_bank(tag)
                 for i in range(2):
-                    stones = slice((2 * k + i) * P, (2 * k + i + 1) * P)
+                    stones = slice((2 * step + i) * P, (2 * step + i + 1) * P)
                     nc.tensor.matmul_mx(
-                        out=bank[:, i * 2 * P : (i + 1) * 2 * P],
+                        out=bank[:, i * GROUP : (i + 1) * GROUP],
                         lhsT=v_w[:, stones].bitcast(FP4X4),
                         lhsT_scale=v_s[:, stones],
-                        rhs=rhs.bitcast(FP8X4),
-                        rhs_scale=rhs_scale,
+                        rhs=words.bitcast(FP8X4),
+                        rhs_scale=scale,
                         start=True,
                         stop=True,
                     )
                 banks.append(bank)
-            if g == 3:
-                ra_sb = picked_all[1][k // 2][:, (k % 2) * BANK : (k % 2 + 1) * BANK]
-            elif k % 2 == 0 or (g, k) == (1, 1):
-                ra_tile = ring.tile([P, BANK], F32, name="ra_sb", tag="ra_sb", bufs=3)
-                ra_sb = ra_tile[:]
-            else:
-                middle = (2 * g - 1) * PAIRS
-                ra_sb = picked_all[0][k // 2][:, middle - BANK // 2 : middle + BANK // 2]
+            ra_sb = ra_staging(g, step)
             nc.scalar.copy(ra_sb, banks[0][:])
-            neg_rd = ring.tile([P, BANK], F32, name="neg_rd", tag="neg_rd", bufs=4)
+            neg_rd = ring.tile([P, BANK], F32, name="neg_rd", tag="neg_rd", bufs=TURN_BUFS)
             nc.scalar.activation(neg_rd[:], banks[2][:], ACT.Copy, scale=-1.0)
-            turned[g, k] = (ra_sb, banks[1], neg_rd)
+            return neg_rd, take_max(banks[1], ra_sb)
 
-        def turned_max(g, k):
-            ra_sb, rb, neg_rd = turned[g, k]
-            m = ring.tile([P, BANK], F32, name="m", tag="m", bufs=4)
-            nc.vector.tensor_tensor(m[:], rb[:], ra_sb, ALU.max)
-            turned[g, k] = (m, neg_rd)
-
-        def turn_back(g, half):
+        def turn_back(g, half, steps):
             for e in range(2):
-                bank = psum.tile([P, BANK], F32, name="hb", tag="hb", bufs=2)
-                for i in range(4):
-                    k, within = divmod(4 * half + i, 2)
-                    cols = slice((2 * within + e) * P, (2 * within + e + 1) * P)
-                    for first, src in ((True, turned[g, k][1]), (False, turned[g, k][0])):
+                bank = new_bank("hb")
+                for i in range(BANK // P):
+                    cols = slice((2 * (i % 2) + e) * P, (2 * (i % 2) + e + 1) * P)
+                    for n, term in enumerate(steps[i // 2]):
                         nc.tensor.matmul(
                             bank[:, i * P : (i + 1) * P],
-                            src[:, cols],
+                            term[:, cols],
                             ident[:],
-                            start=first,
-                            stop=not first,
+                            start=(n == 0),
+                            stop=(n == 1),
                             is_transpose=True,
                         )
                 nc.scalar.copy(h[2 * g + e][:, half * BANK : (half + 1) * BANK], bank[:])
 
-        chunks = {0: ((0, PAIRS),), 1: PARTS}
-        x_codes, x_scales = {}, {}
-        for b in range(2):
-            for j0, j1 in chunks[b]:
-                x_codes[b, j0] = keep.tile([P, j1 - j0], U32, name="x_codes_%d_%d" % (b, j0), align_bytes=64)
-                x_scales[b, j0] = keep.tile([P, j1 - j0], U8, name="x_scales_%d_%d" % (b, j0), align_bytes=64)
-
-        picked_all = [
-            [keep.tile([P, (4 * PAIRS, 3 * PAIRS)[b]], F32, name="picked_%d_%d" % (b, side)) for side in range(2)]
-            for b in range(2)
-        ]
-
-        def picked(b, side, j0, j1):
-            base = PART_BASE[j0] if b == 1 else 0
-            return picked_all[b][side][:, base : base + 4 * (j1 - j0)]
-
         def gather(r, side, j0, j1):
-            b, t = divmod(r, 4)
+            a, t = divmod(r, PACK)
             pos_t = (pos1_t, pos2_t)[side]
             width = j1 - j0
             nc.vector.tensor_copy(
-                picked(b, side, j0, j1)[:, t * width : (t + 1) * width],
+                picked(a, side, j0, j1)[:, t * width : (t + 1) * width],
                 h[r][:].indirect(pos_t[:, j0 // 16 : j1 // 16]),
             )
 
-        x_bf = {}
-
-        def pair_min(b, j0, j1):
-            x_bf[b, j0] = keep.tile([P, j1 - j0, 4], BF16, name="x_bf_%d_%d" % (b, j0), align_bytes=64)
+        def pair_min(a, j0, j1):
+            x_bf[a, j0] = keep.tile([P, j1 - j0, PACK], BF16, name="x_bf_%d_%d" % (a, j0), align_bytes=64)
             nc.vector.tensor_tensor(
-                x_bf[b, j0][:].rearrange("p (c i) t -> p c t i", i=4),
-                picked(b, 0, j0, j1).rearrange("p (t c i) -> p c t i", t=4, i=4),
-                picked(b, 1, j0, j1).rearrange("p (t c i) -> p c t i", t=4, i=4),
+                x_bf[a, j0][:].rearrange("p (c i) t -> p c t i", i=4),
+                picked(a, 0, j0, j1).rearrange("p (t c i) -> p c t i", t=PACK, i=4),
+                picked(a, 1, j0, j1).rearrange("p (t c i) -> p c t i", t=PACK, i=4),
                 ALU.min,
             )
 
-        def quantise_x(b, j0, j1):
-            done = 0
-            for width in (512, 256, 128):
-                if (j1 - j0) & width:
-                    nc.vector.quantize_mx(
-                        out=x_codes[b, j0][:, done : done + width].bitcast(FP8X4),
-                        scales=x_scales[b, j0][:, done : done + width],
-                        in_=x_bf[b, j0][:, done : done + width, :].rearrange("p j t -> p (j t)"),
-                    )
-                    done = done + width
+        def quantise_x(a, j0):
+            nc.vector.quantize_mx(
+                out=x_codes[a, j0][:].bitcast(FP8X4),
+                scales=x_scales[a, j0][:],
+                in_=x_bf[a, j0][:].rearrange("p j t -> p (j t)"),
+            )
 
         y = {}
         y_tags = ("ra", "rb", "rd")
 
         def second_product(a, j0, j1):
-            first = 0 if a == 0 else j0
             for c0 in range(j0, j1, P):
                 last = c0 == PAIRS - P
-                cols = slice(c0 - first, c0 - first + P)
-                for nt in range(N // P):
-                    if a == 0 and (last or nt == 0):
-                        tag = y_tags[nt if last else c0 // P]
-                        bank = psum.tile([P, BANK], F32, name=tag, tag=tag, bufs=2)
+                cols = slice(c0 - j0, c0 - j0 + P)
+                for nt in range(N_TILES):
+                    opens = a == 0 and (last or nt == 0)
+                    if opens:
+                        bank = new_bank(y_tags[nt if last else c0 // P])
                     if a == 0:
                         y[c0, nt] = bank[:, nt * P : (nt + 1) * P]
                     nc.tensor.matmul_mx(
                         out=y[c0, nt],
                         lhsT=w4_w[:, a, 2 * nt * P : 2 * (nt + 1) * P].bitcast(FP4X4),
                         lhsT_scale=w4_s[:, a, nt * P : (nt + 1) * P],
-                        rhs=x_codes[a, first][:, cols].bitcast(FP8X4),
-                        rhs_scale=x_scales[a, first][:, cols],
-                        start=(a == 0 and (last or nt == 0)),
-                        stop=(a == 1 and (last or nt == N // P - 1)),
+                        rhs=x_codes[a, j0][:, cols].bitcast(FP8X4),
+                        rhs_scale=x_scales[a, j0][:, cols],
+                        start=opens,
+                        stop=(a == 1 and (last or nt == N_TILES - 1)),
                     )
 
-        out_v = out.rearrange("(a p) j -> p a j", p=P)
+        out_v = out.rearrange("(nt p) j -> p nt j", p=P)
 
         def finish(j0, j1):
             for c0 in range(j0, j1, P):
-                dist = keep.tile([P, N // P, P], F32, name="dist_%d" % c0)
-                close = keep.tile([P, N // P, P], F32, name="close_%d" % c0)
-                for nt in range(N // P):
-                    nc.scalar.activation(
-                        dist[:, nt, :], y[c0, nt], ACT.Abs, bias=bias[:, nt : nt + 1]
-                    )
+                dist = keep.tile([P, N_TILES, P], F32, name="dist_%d" % c0)
+                close = keep.tile([P, N_TILES, P], F32, name="close_%d" % c0)
+                for nt in range(N_TILES):
+                    nc.scalar.activation(dist[:, nt, :], y[c0, nt], ACT.Abs, bias=bias[:, nt : nt + 1])
                 nc.scalar.activation(close[:], dist[:], ACT.Exp, scale=-1.0)
                 nc.sync.dma_start(out_v[:, :, c0 : c0 + P], close[:])
 
         for r in range(2):
-            for half in range(2):
-                products(r, half)
+            products = [direct_products(r, half) for half in range(2)]
             if r == 0:
-                quantise(1, 0, 1)
+                quantise_weight(1, 1)
+            maxima = [take_max(rb, ra_sb) for ra_sb, rb, rd in products]
             for half in range(2):
-                take_max(r, half)
+                nc.vector.tensor_tensor(
+                    h[r][:, half * BANK : (half + 1) * BANK], maxima[half][:], products[half][2][:], ALU.subtract
+                )
+
+        for g in range(GROUPS - 1):
             for half in range(2):
-                subtract(r, half)
-        for g in range(3):
-            for half in range(2):
-                for k in (2 * half, 2 * half + 1):
-                    turned_products(g + 1, k)
-                    turned_max(g + 1, k)
-                turn_back(g + 1, half)
-                if g < 2:
-                    interleave(half, 1, g, (half, g) in ((1, 0),))
-                for j0, j1 in reversed(chunks[g // 2]):
+                turn_back(g + 1, half, [turned_step(g + 1, step) for step in (2 * half, 2 * half + 1)])
+                if g + 2 < GROUPS:
+                    interleave(half, g + 2)
+                for j0, j1 in reversed(PARTS[g // 2]):
                     gather(2 * g, half, j0, j1)
                     gather(2 * g + 1, half, j0, j1)
-                if g < 2:
-                    quantise(half, 1, g)
+                if g + 2 < GROUPS:
+                    quantise_weight(half, g + 2)
             if g == 1:
                 pair_min(0, 0, PAIRS)
             if g == 2:
-                quantise_x(0, 0, PAIRS)
+                quantise_x(0, 0)
         second_product(0, 0, PAIRS)
-        for j0, j1 in PARTS:
+
+        for j0, j1 in PARTS[1]:
             for side in range(2):
-                gather(6, side, j0, j1)
-                gather(7, side, j0, j1)
+                gather(2 * GROUPS - 2, side, j0, j1)
+                gather(2 * GROUPS - 1, side, j0, j1)
             pair_min(1, j0, j1)
-            quantise_x(1, j0, j1)
+            quantise_x(1, j0)
             second_product(1, j0, j1)
             finish(j0, j1)

from contextlib import ExitStack

import concourse.mybir as mybir
from concourse.masks import make_identity

K, T, S, H, PAIRS, N = 512, 4096, 1024, 1024, 512, 384
FLOPS = 3 * 2 * K * H * S + 2 * H * N * PAIRS

F32 = mybir.dt.float32
BF16 = mybir.dt.bfloat16
I32 = mybir.dt.int32
U32 = mybir.dt.uint32
U16 = mybir.dt.uint16
U8 = mybir.dt.uint8
FP8X4 = mybir.dt.float8_e4m3fn_x4
FP4X4 = mybir.dt.float4_e2m1fn_x4
ALU = mybir.AluOpType
ACT = mybir.ActivationFunctionType

P = 128
PACK = 4
PASS = P * PACK
BANK = 512
QUADS = 4
GROUP = 2 * P
GROUPS = H // GROUP
N_TILES = N // P

PARTS = (((0, PAIRS),), ((0, 256), (256, 384), (384, PAIRS)))
PART_BASE = {0: 512, 256: 256, 384: 0}
PICKED_COLS = (PACK * PAIRS, PART_BASE[0] + PACK * 256)

BANK_BUFS = 2
RA_BUFS = 3
TURN_BUFS = 4


def tile_list_earring_closeness_kernel(
    tc, tab_words, tab_scales, offs, pos1, pos2, w1, w2, w3_words, w3_scales, w4_words, w4_scales, b4, out
):
    nc = tc.nc
    with ExitStack() as ctx:
        keep = ctx.enter_context(tc.tile_pool(name="keep", bufs=1))
        ring = ctx.enter_context(tc.tile_pool(name="ring", bufs=2))
        psum = ctx.enter_context(tc.psum_pool(name="psum", bufs=1))

        offs_t = keep.tile([P, S // 16], U16, name="offs_t")
        pos1_t = keep.tile([P, PAIRS // 16], U16, name="pos1_t")
        pos2_t = keep.tile([P, PAIRS // 16], U16, name="pos2_t")
        tab_w = keep.tile([P, T], U16, name="tab_w", align_bytes=64)
        tab_s = keep.tile([P, T], U8, name="tab_s", align_bytes=64)
        v_w = keep.tile([P, S], U16, name="v_w", align_bytes=64)
        v_s = keep.tile([P, S], U8, name="v_s", align_bytes=64)
        w3_s_raw = ring.tile([P, H], U8, name="w3_s_raw", tag="rows", bufs=1, align_bytes=64)
        bias = keep.tile([P, N_TILES], F32, name="bias")

        nc.vector.memset(tab_s[:].bitcast(I32), 0)
        nc.gpsimd.memset(w3_s_raw[:].bitcast(I32), 0)

        nc.sync.dma_start(offs_t[:], offs)
        ident = keep.tile([P, P], F32, name="ident")
        nc.sync.dma_start(pos1_t[:], pos1)
        nc.sync.dma_start(pos2_t[:], pos2)
        nc.sync.dma_start(tab_w[:].bitcast(I32), tab_words[0].bitcast(I32))
        for q in range(QUADS):
            nc.scalar.dma_start(
                tab_s[32 * q : 32 * q + 4, :].bitcast(I32), tab_scales[0, 4 * q : 4 * q + 4, :].bitcast(I32)
            )
        for q in range(QUADS):
            nc.gpsimd.dma_start(
                w3_s_raw[32 * q : 32 * q + 4, :].bitcast(I32), w3_scales[0, 4 * q : 4 * q + 4, :].bitcast(I32)
            )

        def load_columns(w, a):
            raw = ring.tile([P, PACK, PASS], F32, name="raw", tag="raw", bufs=2)
            nc.sync.dma_start(raw[:], w[:, a * PASS : (a + 1) * PASS].rearrange("(p i) c -> p i c", i=PACK))
            return raw

        raws = {}
        raws[0, 0] = load_columns(w1, 0)
        raws[1, 0] = load_columns(w2, 0)
        w3_w_raw = ring.tile([P, H], I32, name="w3_w_raw", tag="words", bufs=1, align_bytes=64)
        nc.sync.dma_start(w3_w_raw[:], w3_words[0].rearrange("p c i -> p (c i)").bitcast(I32))

        with nc.allow_non_contiguous_dma(reason="one bias value for each partition"):
            nc.gpsimd.dma_start(bias[:], b4.rearrange("(c p) -> p c", p=P))

        make_identity(nc, ident[:])
        nc.vector.tensor_copy(v_w[:], tab_w[:].indirect(offs_t[:]))
        nc.vector.tensor_copy(v_s[:], tab_s[:].indirect(offs_t[:]))

        grouped, codes, scales = {}, {}, {}
        for w in range(2):
            for g in range(GROUPS):
                grouped[w, g] = keep.tile(
                    [P, 2, P, PACK], BF16, name="grouped", tag="grouped_%d_%d" % (w, g), align_bytes=64
                )
                codes[w, g] = keep.tile([P, GROUP], U32, name="codes_%d_%d" % (w, g), align_bytes=64)
                scales[w, g] = keep.tile([P, GROUP], U8, name="scales_%d_%d" % (w, g), align_bytes=64)

        def interleave(w, g):
            a, u = divmod(g, 2)
            src = raws[w, a][:].rearrange("p i (m t) -> p m i t", t=PACK)[:, :, :, 2 * u : 2 * u + 2]
            nc.scalar.copy(grouped[w, g][:].rearrange("p e m i -> p m i e"), src)

        def quantise_weight(w, g):
            nc.vector.quantize_mx(
                out=codes[w, g][:].bitcast(FP8X4),
                scales=scales[w, g][:],
                in_=grouped[w, g][:].rearrange("p e m i -> p (e m i)"),
            )

        w3_w = keep.tile([P, H], I32, name="w3_w", align_bytes=64)
        interleave(0, 0)
        interleave(0, 1)
        interleave(1, 0)
        quantise_weight(0, 0)
        w3_s = keep.tile([P, H], U8, name="w3_s", tag="grouped_0_0", align_bytes=64)
        nc.vector.tensor_copy(
            w3_s[:].rearrange("p (a t m) -> p a t m", a=2, t=PACK),
            w3_s_raw[:].rearrange("p (a m t) -> p a t m", a=2, t=PACK),
        )
        quantise_weight(1, 0)
        nc.vector.tensor_copy(
            w3_w[:].rearrange("p (a t m) -> p a m t", a=2, t=PACK),
            w3_w_raw[:].rearrange("p (a m t) -> p a m t", a=2, t=PACK),
        )
        interleave(1, 1)
        quantise_weight(0, 1)

        raws[0, 1] = load_columns(w1, 1)
        raws[1, 1] = load_columns(w2, 1)
        w4_w = ring.tile([P, 2, 2 * N], U8, name="w4_w", tag="words", bufs=1, align_bytes=64)
        nc.sync.dma_start(w4_w[:].bitcast(I32), w4_words.rearrange("a p c -> p a c").bitcast(I32))
        w4_s = ring.tile([P, 2, N], U8, name="w4_s", tag="rows", bufs=1, align_bytes=64)
        nc.gpsimd.memset(w4_s[:].bitcast(I32), 0)
        for q in range(QUADS):
            nc.sync.dma_start(
                w4_s[32 * q : 32 * q + 4, :, :].bitcast(I32),
                w4_scales[:, 4 * q : 4 * q + 4, :].rearrange("a r n -> r a n").bitcast(I32),
            )

        h = [keep.tile([P, S], F32, name="h_%d" % r) for r in range(H // P)]

        def readings(g, cols):
            w3_cols = slice(g * GROUP + cols.start, g * GROUP + cols.stop)
            return (
                ("ra", codes[0, g][:, cols], scales[0, g][:, cols]),
                ("rb", codes[1, g][:, cols], scales[1, g][:, cols]),
                ("rd", w3_w[:, w3_cols], w3_s[:, w3_cols]),
            )

        def new_bank(tag):
            return psum.tile([P, BANK], F32, name=tag, tag=tag, bufs=BANK_BUFS)

        def new_ra():
            return ring.tile([P, BANK], F32, name="ra_sb", tag="ra_sb", bufs=RA_BUFS)

        def take_max(rb, ra_sb):
            larger = ring.tile([P, BANK], F32, name="larger", tag="larger", bufs=TURN_BUFS)
            nc.vector.tensor_tensor(larger[:], rb[:], ra_sb, ALU.max)
            return larger

        def direct_products(r, half):
            stones = slice(half * BANK, (half + 1) * BANK)
            banks = []
            for tag, words, scale in readings(0, slice(r * P, (r + 1) * P)):
                bank = new_bank(tag)
                nc.tensor.matmul_mx(
                    out=bank[:],
                    lhsT=words.bitcast(FP8X4),
                    lhsT_scale=scale,
                    rhs=v_w[:, stones].bitcast(FP4X4),
                    rhs_scale=v_s[:, stones],
                    start=True,
                    stop=True,
                )
                banks.append(bank)
            ra_sb = new_ra()
            nc.scalar.copy(ra_sb[:], banks[0][:])
            return ra_sb[:], banks[1], banks[2]

        x_codes, x_scales, x_bf = {}, {}, {}
        for a in range(2):
            for j0, j1 in PARTS[a]:
                x_codes[a, j0] = keep.tile([P, j1 - j0], U32, name="x_codes_%d_%d" % (a, j0), align_bytes=64)
                x_scales[a, j0] = keep.tile([P, j1 - j0], U8, name="x_scales_%d_%d" % (a, j0), align_bytes=64)

        picked_tiles = [
            [keep.tile([P, PICKED_COLS[a]], F32, name="picked_%d_%d" % (a, side)) for side in range(2)]
            for a in range(2)
        ]

        def picked(a, side, j0, j1):
            base = PART_BASE[j0] if a == 1 else 0
            return picked_tiles[a][side][:, base : base + PACK * (j1 - j0)]

        def ra_staging(g, step):
            side = step // 2
            if g == GROUPS - 1:
                return picked_tiles[1][side][:, (step % 2) * BANK : (step % 2 + 1) * BANK]
            if step % 2 == 0 or (g == 1 and side == 0):
                ra_sb = new_ra()
                return ra_sb[:]
            border = (2 * (g - 1) + 1) * PAIRS
            return picked_tiles[0][side][:, border - BANK // 2 : border + BANK // 2]

        def turned_step(g, step):
            banks = []
            for tag, words, scale in readings(g, slice(0, GROUP)):
                bank = new_bank(tag)
                for i in range(2):
                    stones = slice((2 * step + i) * P, (2 * step + i + 1) * P)
                    nc.tensor.matmul_mx(
                        out=bank[:, i * GROUP : (i + 1) * GROUP],
                        lhsT=v_w[:, stones].bitcast(FP4X4),
                        lhsT_scale=v_s[:, stones],
                        rhs=words.bitcast(FP8X4),
                        rhs_scale=scale,
                        start=True,
                        stop=True,
                    )
                banks.append(bank)
            ra_sb = ra_staging(g, step)
            nc.scalar.copy(ra_sb, banks[0][:])
            neg_rd = ring.tile([P, BANK], F32, name="neg_rd", tag="neg_rd", bufs=TURN_BUFS)
            nc.scalar.activation(neg_rd[:], banks[2][:], ACT.Copy, scale=-1.0)
            return neg_rd, take_max(banks[1], ra_sb)

        def turn_back(g, half, steps):
            for e in range(2):
                bank = new_bank("hb")
                for i in range(BANK // P):
                    cols = slice((2 * (i % 2) + e) * P, (2 * (i % 2) + e + 1) * P)
                    for n, term in enumerate(steps[i // 2]):
                        nc.tensor.matmul(
                            bank[:, i * P : (i + 1) * P],
                            term[:, cols],
                            ident[:],
                            start=(n == 0),
                            stop=(n == 1),
                            is_transpose=True,
                        )
                nc.scalar.copy(h[2 * g + e][:, half * BANK : (half + 1) * BANK], bank[:])

        def gather(r, side, j0, j1):
            a, t = divmod(r, PACK)
            pos_t = (pos1_t, pos2_t)[side]
            width = j1 - j0
            nc.vector.tensor_copy(
                picked(a, side, j0, j1)[:, t * width : (t + 1) * width],
                h[r][:].indirect(pos_t[:, j0 // 16 : j1 // 16]),
            )

        def pair_min(a, j0, j1):
            x_bf[a, j0] = keep.tile([P, j1 - j0, PACK], BF16, name="x_bf_%d_%d" % (a, j0), align_bytes=64)
            nc.vector.tensor_tensor(
                x_bf[a, j0][:].rearrange("p (c i) t -> p c t i", i=4),
                picked(a, 0, j0, j1).rearrange("p (t c i) -> p c t i", t=PACK, i=4),
                picked(a, 1, j0, j1).rearrange("p (t c i) -> p c t i", t=PACK, i=4),
                ALU.min,
            )

        def quantise_x(a, j0):
            nc.vector.quantize_mx(
                out=x_codes[a, j0][:].bitcast(FP8X4),
                scales=x_scales[a, j0][:],
                in_=x_bf[a, j0][:].rearrange("p j t -> p (j t)"),
            )

        y = {}
        y_tags = ("ra", "rb", "rd")

        def second_product(a, j0, j1):
            for c0 in range(j0, j1, P):
                last = c0 == PAIRS - P
                cols = slice(c0 - j0, c0 - j0 + P)
                for nt in range(N_TILES):
                    opens = a == 0 and (last or nt == 0)
                    if opens:
                        bank = new_bank(y_tags[nt if last else c0 // P])
                    if a == 0:
                        y[c0, nt] = bank[:, nt * P : (nt + 1) * P]
                    nc.tensor.matmul_mx(
                        out=y[c0, nt],
                        lhsT=w4_w[:, a, 2 * nt * P : 2 * (nt + 1) * P].bitcast(FP4X4),
                        lhsT_scale=w4_s[:, a, nt * P : (nt + 1) * P],
                        rhs=x_codes[a, j0][:, cols].bitcast(FP8X4),
                        rhs_scale=x_scales[a, j0][:, cols],
                        start=opens,
                        stop=(a == 1 and (last or nt == N_TILES - 1)),
                    )

        out_v = out.rearrange("(nt p) j -> p nt j", p=P)

        def finish(j0, j1):
            for c0 in range(j0, j1, P):
                dist = keep.tile([P, N_TILES, P], F32, name="dist_%d" % c0)
                close = keep.tile([P, N_TILES, P], F32, name="close_%d" % c0)
                for nt in range(N_TILES):
                    nc.scalar.activation(dist[:, nt, :], y[c0, nt], ACT.Abs, bias=bias[:, nt : nt + 1])
                nc.scalar.activation(close[:], dist[:], ACT.Exp, scale=-1.0)
                nc.sync.dma_start(out_v[:, :, c0 : c0 + P], close[:])

        for r in range(2):
            products = [direct_products(r, half) for half in range(2)]
            if r == 0:
                quantise_weight(1, 1)
            maxima = [take_max(rb, ra_sb) for ra_sb, rb, rd in products]
            for half in range(2):
                nc.vector.tensor_tensor(
                    h[r][:, half * BANK : (half + 1) * BANK], maxima[half][:], products[half][2][:], ALU.subtract
                )

        for g in range(GROUPS - 1):
            for half in range(2):
                turn_back(g + 1, half, [turned_step(g + 1, step) for step in (2 * half, 2 * half + 1)])
                if g + 2 < GROUPS:
                    interleave(half, g + 2)
                for j0, j1 in reversed(PARTS[g // 2]):
                    gather(2 * g, half, j0, j1)
                    gather(2 * g + 1, half, j0, j1)
                if g + 2 < GROUPS:
                    quantise_weight(half, g + 2)
            if g == 1:
                pair_min(0, 0, PAIRS)
            if g == 2:
                quantise_x(0, 0)
        second_product(0, 0, PAIRS)

        for j0, j1 in PARTS[1]:
            for side in range(2):
                gather(2 * GROUPS - 2, side, j0, j1)
                gather(2 * GROUPS - 1, side, j0, j1)
            pair_min(1, j0, j1)
            quantise_x(1, j0)
            second_product(1, j0, j1)
            finish(j0, j1)
